import numpy as np
import ml_dtypes


def mxq(x, axis, fmt="e4m3"):
    dtype, down = {"e4m3": (ml_dtypes.float8_e4m3fn, 7), "e5m2": (ml_dtypes.float8_e5m2, 14)}[fmt]
    v = np.moveaxis(np.asarray(x, np.float32).astype(ml_dtypes.bfloat16).astype(np.float64), axis, -1)
    blocks = v.reshape(v.shape[:-1] + (-1, 32))
    amax = np.abs(blocks).max(-1, keepdims=True)
    byte = np.maximum(np.where(amax > 0, np.frexp(amax)[1] - 1 + 127, 0) - down, 1)
    scale = np.exp2(byte - 127.0)
    codes = (blocks / scale).astype(np.float32).astype(dtype).astype(np.float64)
    return np.moveaxis((codes * scale).reshape(v.shape), -1, axis)


WIDE = False


def mx_kscale(k):
    if not WIDE:
        return np.ones(k)
    levels = np.array([10, -10, 5, -5, 0])
    if k % 512:
        return np.exp2(np.random.permutation(np.resize(levels, k // 32))).repeat(32)
    a = np.empty((k // 512, 16))
    for p in range(k // 512):
        a[p, :8] = np.random.permutation(np.resize(levels, 8))
        for g in range(8):
            far = levels[np.abs(levels - a[p, g]) >= 10]
            a[p, g + 8] = far[np.random.randint(len(far))]
    return np.exp2(a.ravel()).repeat(32)


def f64(x):
    return np.asarray(x).astype(np.float64)


def striped8(idx):
    return np.asarray(idx).reshape(8, -1, 16).transpose(0, 2, 1).reshape(128, -1).astype(np.uint16)


def unstriped8(offs):
    return offs.reshape(8, 16, -1).transpose(0, 2, 1).reshape(8, -1).astype(np.int64)


def pick8(x, idx, run):
    r = np.arange(len(x))
    return x[r[:, None], idx[r % (8 * run) // run]]


E2M1 = np.array([0.0, 0.5, 1.0, 1.5, 2.0, 3.0, 4.0, 6.0, -0.0, -0.5, -1.0, -1.5, -2.0, -3.0, -4.0, -6.0])


def pack_weight(w, fmt):
    k, n = w.shape
    w = f64(np.asarray(w, np.float32).astype(ml_dtypes.bfloat16)).reshape(k // 32, 32, n)
    amax = np.abs(w).max(1)
    if fmt == "e4m3":
        byte = np.frexp(amax)[1] - 1 + 127 - 7
    else:
        mant, ex = np.frexp(amax / 6.0)
        byte = np.where(mant > 0.5, ex, ex - 1) + 127
    byte = np.clip(np.where(amax > 0, byte, 1), 1, 254)
    scaled = (w * np.exp2(127.0 - byte)[:, None, :]).reshape(k, n).astype(np.float32)
    by_word = np.ascontiguousarray(scaled.reshape(k // 512, 128, 4, n).transpose(0, 1, 3, 2))
    if fmt == "e4m3":
        words = by_word.astype(ml_dtypes.float8_e4m3fn).view(np.uint8)
    else:
        c = by_word.astype(ml_dtypes.float4_e2m1fn).view(np.uint8) & 0xF
        words = (c[..., 0::2] | (c[..., 1::2] << 4)).reshape(k // 512, 128, 2 * n)
    return np.ascontiguousarray(words), np.ascontiguousarray(byte.astype(np.uint8).reshape(k // 512, 16, n))


def unpack_weight(words, scales, fmt):
    g, _, n = scales.shape
    words = np.ascontiguousarray(words).reshape(g, 128, n, -1)
    if fmt == "e4m3":
        vals = words.view(ml_dtypes.float8_e4m3fn).astype(np.float64)
    else:
        nib = np.empty((g, 128, n, 4), np.uint8)
        nib[..., 0::2] = words & 0xF
        nib[..., 1::2] = words >> 4
        vals = E2M1[nib]
    vals = vals * np.repeat(np.exp2(scales.astype(np.float64) - 127.0), 8, axis=1)[..., None]
    return vals.transpose(0, 1, 3, 2).reshape(g * 512, n)


D, T, I, J, Q, E = 512, 1024, 512, 256, 512, 256


def setup_inputs():
    n = np.random.standard_normal
    idx = np.stack([np.random.permutation(T)[:J] for _ in range(8)])
    idx2 = np.stack([np.random.permutation(T)[:J] for _ in range(8)])
    idx3 = np.stack([np.random.permutation(T)[:I] for _ in range(8)])
    idx4 = np.stack([np.random.permutation(T)[:J] for _ in range(8)])
    idx5 = np.stack([np.random.permutation(T)[:I] for _ in range(8)])
    fd = mx_kscale(D)
    fq = mx_kscale(Q)
    cachep = pack_weight(n((D, T)) / fd[:, None], "e4m3")
    mixp = pack_weight(n((Q, E)) * 1.0 / np.sqrt(Q) / fq[:, None], "e2m1")
    return {
        "query": (n((D, Q)) * 1.0 / np.sqrt(D) * fd[:, None]).astype(np.float32),
        "cache_words": cachep[0],
        "cache_scales": cachep[1],
        "rowf": (np.random.uniform(0.5, 2.0, (Q, 1)) * fq[:, None]).astype(np.float32),
        "mix_words": mixp[0],
        "mix_scales": mixp[1],
        "offs": striped8(idx),
        "offs2": striped8(idx2),
        "offs3": striped8(idx3),
        "offs4": striped8(idx4),
        "offs5": striped8(idx5),
    }


def reference(query, cache_words, cache_scales, rowf, mix_words, mix_scales, offs, offs2, offs3, offs4, offs5):
    idx = unstriped8(offs)
    idx2 = unstriped8(offs2)
    idx3 = unstriped8(offs3)
    idx4 = unstriped8(offs4)
    idx5 = unstriped8(offs5)
    cacheu = unpack_weight(cache_words, cache_scales, "e4m3")
    mixu = unpack_weight(mix_words, mix_scales, "e2m1")
    queryq = mxq(f64(query), 0, "e4m3")
    a = queryq.T @ cacheu
    w = np.concatenate([pick8(a, idx, 64), pick8(a, idx2, 64)], axis=1)
    f1 = np.zeros((Q, T))
    f1[np.arange(Q)[:, None], idx3[np.arange(Q) % 512 // 64]] = w
    c1 = a - f1
    v = pick8(c1, idx4, 64) - pick8(a, idx, 64)
    f2 = np.zeros((Q, T))
    f2[np.arange(Q)[:, None], idx2[np.arange(Q) % 512 // 64]] = v
    c2 = np.maximum(c1, f2)
    g = pick8(c2, idx5, 64)
    gw = g * f64(rowf)
    gwq = mxq(gw, 0, "e4m3")
    y = mixu.T @ gwq
    return y

@@ -1,0 +1,223 @@
+from contextlib import ExitStack
+
+import concourse.mybir as mybir
+
+D, T, I, J, Q, E = 512, 1024, 512, 256, 512, 256
+FLOPS = 2 * D * Q * T + 2 * Q * E * I
+
+F32 = mybir.dt.float32
+BF16 = mybir.dt.bfloat16
+I32 = mybir.dt.int32
+U32 = mybir.dt.uint32
+U16 = mybir.dt.uint16
+U8 = mybir.dt.uint8
+FP8X4 = mybir.dt.float8_e4m3fn_x4
+FP4X4 = mybir.dt.float4_e2m1fn_x4
+ALU = mybir.AluOpType
+COPY = mybir.ActivationFunctionType.Copy
+
+P = 128
+PACK = 4
+BANK = 512
+HALF = 256
+
+
+def load_scale_rows(queue, plane, rows):
+    for quad in range(4):
+        queue.dma_start(
+            out=plane[32 * quad : 32 * quad + 4, :].bitcast(I32),
+            in_=rows[4 * quad : 4 * quad + 4, :].bitcast(I32),
+        )
+
+
+def tile_attend_halfruns_one_mixed_kernel(
+    tc, query, cache_words, cache_scales, rowf, mix_words, mix_scales, offs, offs2, offs3, offs4, offs5, out
+):
+    nc = tc.nc
+    with ExitStack() as ctx:
+        lists = ctx.enter_context(tc.tile_pool(name="lists", bufs=1))
+        sb = ctx.enter_context(tc.tile_pool(name="sb", bufs=1))
+        psum = ctx.enter_context(tc.psum_pool(name="psum", bufs=1))
+
+        cache_plane = sb.tile([P, T], U8, name="cache_plane", align_bytes=64)
+        mix_plane = sb.tile([P, E], U8, name="mix_plane", align_bytes=64)
+        nc.vector.memset(cache_plane[:].bitcast(I32), 0)
+        nc.vector.memset(mix_plane[:].bitcast(I32), 0)
+
+        query_pj = query.rearrange("(p j) q -> p j q", j=PACK)
+        raw = [sb.tile([P, PACK, HALF], F32, name="raw%d" % c) for c in range(2)]
+        for c in range(2):
+            nc.sync.dma_start(out=raw[c][:], in_=query_pj[:, :, c * HALF : (c + 1) * HALF])
+        load_scale_rows(nc.scalar, cache_plane, cache_scales[0])
+        words_flat = cache_words[0].rearrange("p n t -> p (n t)")
+        keys = [sb.tile([P, BANK], I32, name="keys%d" % b, align_bytes=64) for b in range(2)]
+        for b in range(2):
+            nc.sync.dma_start(out=keys[b][:], in_=words_flat[:, b * BANK * PACK : (b + 1) * BANK * PACK].bitcast(I32))
+        factor = sb.tile([P, PACK], F32, name="factor")
+        nc.sync.dma_start(out=factor[:], in_=rowf.rearrange("(p r) o -> p (r o)", r=PACK))
+
+        l1 = lists.tile([P, J // 16], U16, name="l1")
+        l2 = lists.tile([P, J // 16], U16, name="l2")
+        l3 = lists.tile([P, I // 16], U16, name="l3")
+        l4 = lists.tile([P, J // 16], U16, name="l4")
+        l5 = lists.tile([P, I // 16], U16, name="l5")
+        nc.sync.dma_start(l1[:], offs)
+        nc.sync.dma_start(l3[:], offs3)
+        nc.sync.dma_start(l2[:], offs2)
+        nc.sync.dma_start(l4[:], offs4)
+        nc.sync.dma_start(l5[:], offs5)
+        mix_codes = sb.tile([P, 2 * E], U8, name="mix_codes", align_bytes=64)
+        nc.sync.dma_start(out=mix_codes[:].bitcast(I32), in_=mix_words[0].bitcast(I32))
+        load_scale_rows(nc.sync, mix_plane, mix_scales[0])
+
+        f1 = [sb.tile([P, T], F32, name="f1_%d" % s) for s in range(2)]
+        f2 = [sb.tile([P, T], F32, name="f2_%d" % s) for s in range(2)]
+        for window in (f1[0], f1[1], f2[0], f2[1]):
+            nc.vector.memset(window[:], 0.0)
+
+        M = HALF // PACK
+        qb0 = sb.tile([P, P, PACK], BF16, name="qb0", align_bytes=64)
+        qb1 = sb.tile([P, PACK - 1, P, PACK], BF16, name="qb1", align_bytes=64)
+        qb1_m = qb1[:].rearrange("p r m j -> p m r j")
+        src = [raw[c][:].rearrange("p j (m r) -> p m r j", r=PACK) for c in range(2)]
+        nc.vector.tensor_copy(out=qb0[:, 0:M, :], in_=src[0][:, :, 0, :])
+        nc.scalar.copy(out=qb1_m[:, 0:M], in_=src[0][:, :, 1:PACK, :])
+        nc.vector.tensor_copy(out=qb0[:, M : 2 * M, :], in_=src[1][:, :, 0, :])
+        nc.scalar.copy(out=qb1_m[:, M : 2 * M], in_=src[1][:, :, 1:PACK, :])
+        qc0 = sb.tile([P, P], U32, name="qc0", align_bytes=64)
+        qs0 = sb.tile([P, P], U8, name="qs0", align_bytes=64)
+        qc1 = sb.tile([P, (PACK - 1) * P], U32, name="qc1", align_bytes=64)
+        qs1 = sb.tile([P, (PACK - 1) * P], U8, name="qs1", align_bytes=64)
+        nc.vector.quantize_mx(out=qc0[:].bitcast(FP8X4), scales=qs0[:], in_=qb0[:].rearrange("p m j -> p (m j)"))
+        nc.vector.quantize_mx(out=qc1[:].bitcast(FP8X4), scales=qs1[:], in_=qb1[:].rearrange("p r m j -> p (r m j)"))
+
+        spread = {}
+        for r, width in ((0, I), (3, HALF)):
+            spread[r] = sb.tile([P, width], F32, name="spread%d" % r)
+            nc.vector.tensor_copy(out=spread[r][:], in_=factor[:, r : r + 1].to_broadcast([P, width]))
+
+        banks = {}
+        for r in range(PACK):
+            if r == 0:
+                codes, plane = qc0[:], qs0[:]
+            else:
+                codes, plane = qc1[:, (r - 1) * P : r * P], qs1[:, (r - 1) * P : r * P]
+            for b in range(2):
+                banks[r, b] = psum.tile([P, BANK], F32, name="bank%d" % (2 * r + b))
+                nc.tensor.matmul_mx(
+                    out=banks[r, b][:],
+                    lhsT=codes.bitcast(FP8X4),
+                    lhsT_scale=plane,
+                    rhs=keys[b][:].bitcast(FP8X4),
+                    rhs_scale=cache_plane[:, b * BANK : (b + 1) * BANK],
+                    start=True,
+                    stop=True,
+                )
+
+        a = [sb.tile([P, T], F32, name="a%d" % r) for r in range(PACK)]
+        w = [sb.tile([P, I], F32, name="w%d" % r) for r in range(PACK)]
+        c1 = [sb.tile([P, T], F32, name="c1_%d" % r) for r in range(PACK)]
+        v = [sb.tile([P, J], F32, name="v%d" % r) for r in range(PACK)]
+        c2 = {}
+        gw = sb.tile([P, PACK, I], F32, name="gw")
+
+        def leave_v(r, b):
+            nc.vector.tensor_copy(out=a[r][:, b * BANK : (b + 1) * BANK], in_=banks[r, b][:])
+
+        def leave_s(r, b):
+            nc.scalar.copy(out=a[r][:, b * BANK : (b + 1) * BANK], in_=banks[r, b][:])
+
+        def w_low(r):
+            nc.vector.tensor_copy(w[r][:, 0:J], a[r][:].indirect(l1[:]))
+
+        def w_high(r):
+            nc.vector.tensor_copy(w[r][:, J:I], a[r][:].indirect(l2[:]))
+
+        def put_w(r):
+            nc.scalar.activation(f1[r % 2][:].indirect(l3[:]), w[r][:], COPY)
+
+        def make_c1(r):
+            nc.vector.tensor_tensor(c1[r][:], a[r][:], f1[r % 2][:], ALU.subtract)
+
+        def make_v(r):
+            nc.vector.tensor_tensor(v[r][:], c1[r][:].indirect(l4[:]), w[r][:, 0:J], ALU.subtract)
+
+        def put_v(r):
+            nc.scalar.activation(f2[r % 2][:].indirect(l2[:]), v[r][:], COPY)
+
+        def make_c2(r):
+            c2[r] = sb.tile([P, T], F32, name="w3" if r == 2 else "c2_%d" % r)
+            nc.vector.tensor_tensor(c2[r][:], c1[r][:], f2[r % 2][:], ALU.max)
+
+        def gw_vector(r):
+            nc.vector.tensor_tensor(gw[:, r, :], c2[r][:].indirect(l5[:]), spread[r][:], ALU.mult)
+
+        leave_s(0, 0)
+        leave_v(0, 1)
+        w_low(0)
+        leave_s(1, 0)
+        nc.scalar.activation(f1[0][:].indirect(l3[:, 0:16]), w[0][:, 0:J], COPY)
+        w_high(0)
+        nc.scalar.activation(f1[0][:].indirect(l3[:, 16:32]), w[0][:, J:I], COPY)
+        leave_v(1, 1)
+        w_low(1)
+        w_high(1)
+        put_w(1)
+        leave_v(2, 0)
+        leave_v(2, 1)
+        make_c1(0)
+        w_low(2)
+        make_v(0)
+        put_v(0)
+        w_high(2)
+        put_w(2)
+        make_c1(1)
+        leave_v(3, 0)
+        make_v(1)
+        put_v(1)
+        leave_v(3, 1)
+        make_c2(0)
+        w_low(3)
+        w_high(3)
+        put_w(3)
+        make_c1(2)
+        make_c2(1)
+        nc.scalar.activation(gw[:, 1, :], c2[1][:].indirect(l5[:]), COPY, scale=factor[:, 1:2])
+        make_v(2)
+        put_v(2)
+        gw_vector(0)
+        make_c1(3)
+        make_v(3)
+        put_v(3)
+        make_c2(2)
+        nc.scalar.activation(gw[:, 2, :], c2[2][:].indirect(l5[:]), COPY, scale=factor[:, 2:3])
+        make_c2(3)
+        nc.vector.tensor_tensor(gw[:, 3, 0:HALF], c2[3][:].indirect(l5[:, 0:16]), spread[3][:], ALU.mult)
+        nc.scalar.activation(gw[:, 3, HALF:I], c2[3][:].indirect(l5[:, 16:32]), COPY, scale=factor[:, 3:4])
+
+        gw_ir = gw[:].rearrange("p r i -> p i r")
+        out_b = out.rearrange("(b p) i -> p b i", p=P)
+        gb = [sb.tile([P, HALF, PACK], BF16, name="gb%d" % h, align_bytes=64) for h in range(2)]
+        nc.vector.tensor_copy(out=gb[0][:], in_=gw_ir[:, 0:HALF, :])
+        nc.scalar.copy(out=gb[1][:], in_=gw_ir[:, HALF:I, :])
+        for h in range(2):
+            gc = sb.tile([P, HALF], U32, name="gc%d" % h, align_bytes=64)
+            gs = sb.tile([P, HALF], U8, name="gs%d" % h, align_bytes=64)
+            nc.vector.quantize_mx(out=gc[:].bitcast(FP8X4), scales=gs[:], in_=gb[h][:].rearrange("p i r -> p (i r)"))
+            res = sb.tile([P, 2, HALF], F32, name="res%d" % h)
+            for b in range(2):
+                acc = psum.tile([P, BANK], F32, name="bank%d" % (2 * h + b))
+                nc.tensor.matmul_mx(
+                    out=acc[:, 0:HALF],
+                    lhsT=mix_codes[:, 2 * P * b : 2 * P * (b + 1)].bitcast(FP4X4),
+                    lhsT_scale=mix_plane[:, P * b : P * (b + 1)],
+                    rhs=gc[:].bitcast(FP8X4),
+                    rhs_scale=gs[:],
+                    start=True,
+                    stop=True,
+                )
+                if b == 0:
+                    nc.vector.tensor_copy(out=res[:, b, :], in_=acc[:, 0:HALF])
+                else:
+                    nc.scalar.copy(out=res[:, b, :], in_=acc[:, 0:HALF])
+            nc.sync.dma_start(out=out_b[:, :, h * HALF : (h + 1) * HALF], in_=res[:])

@@ -20,6 +20,7 @@ P = 128
 PACK = 4
 BANK = 512
 HALF = 256
+FIRST_BANK = (0, 4, 6, 0)
 
 
 def load_scale_rows(queue, plane, rows):
@@ -44,17 +45,18 @@ def tile_attend_halfruns_one_mixed_kernel(
         nc.vector.memset(cache_plane[:].bitcast(I32), 0)
         nc.vector.memset(mix_plane[:].bitcast(I32), 0)
 
+        factor = sb.tile([P, PACK], F32, name="factor")
+        nc.sync.dma_start(out=factor[:], in_=rowf.rearrange("(p r) o -> p (r o)", r=PACK))
+        scale_rows = sb.tile([4, 4, T // 4], I32, name="scale_rows")
+        nc.sync.dma_start(out=scale_rows[:], in_=cache_scales[0].bitcast(I32).rearrange("(quad f) c -> f quad c", f=4))
         query_pj = query.rearrange("(p j) q -> p j q", j=PACK)
         raw = [sb.tile([P, PACK, HALF], F32, name="raw%d" % c) for c in range(2)]
         for c in range(2):
             nc.sync.dma_start(out=raw[c][:], in_=query_pj[:, :, c * HALF : (c + 1) * HALF])
-        load_scale_rows(nc.scalar, cache_plane, cache_scales[0])
         words_flat = cache_words[0].rearrange("p n t -> p (n t)")
         keys = [sb.tile([P, BANK], I32, name="keys%d" % b, align_bytes=64) for b in range(2)]
         for b in range(2):
             nc.sync.dma_start(out=keys[b][:], in_=words_flat[:, b * BANK * PACK : (b + 1) * BANK * PACK].bitcast(I32))
-        factor = sb.tile([P, PACK], F32, name="factor")
-        nc.sync.dma_start(out=factor[:], in_=rowf.rearrange("(p r) o -> p (r o)", r=PACK))
 
         l1 = lists.tile([P, J // 16], U16, name="l1")
         l2 = lists.tile([P, J // 16], U16, name="l2")
@@ -70,62 +72,71 @@ def tile_attend_halfruns_one_mixed_kernel(
         nc.sync.dma_start(out=mix_codes[:].bitcast(I32), in_=mix_words[0].bitcast(I32))
         load_scale_rows(nc.sync, mix_plane, mix_scales[0])
 
-        f1 = [sb.tile([P, T], F32, name="f1_%d" % s) for s in range(2)]
+        f1 = [sb.tile([P, T], F32, name="f1_%d" % s, align_bytes=64) for s in range(2)]
         f2 = [sb.tile([P, T], F32, name="f2_%d" % s) for s in range(2)]
-        for window in (f1[0], f1[1], f2[0], f2[1]):
-            nc.vector.memset(window[:], 0.0)
+        for window in f1 + f2:
+            nc.vector.memset(window[:].bitcast(I32), 0)
 
-        M = HALF // PACK
-        qb0 = sb.tile([P, P, PACK], BF16, name="qb0", align_bytes=64)
-        qb1 = sb.tile([P, PACK - 1, P, PACK], BF16, name="qb1", align_bytes=64)
-        qb1_m = qb1[:].rearrange("p r m j -> p m r j")
-        src = [raw[c][:].rearrange("p j (m r) -> p m r j", r=PACK) for c in range(2)]
-        nc.vector.tensor_copy(out=qb0[:, 0:M, :], in_=src[0][:, :, 0, :])
-        nc.scalar.copy(out=qb1_m[:, 0:M], in_=src[0][:, :, 1:PACK, :])
-        nc.vector.tensor_copy(out=qb0[:, M : 2 * M, :], in_=src[1][:, :, 0, :])
-        nc.scalar.copy(out=qb1_m[:, M : 2 * M], in_=src[1][:, :, 1:PACK, :])
-        qc0 = sb.tile([P, P], U32, name="qc0", align_bytes=64)
-        qs0 = sb.tile([P, P], U8, name="qs0", align_bytes=64)
-        qc1 = sb.tile([P, (PACK - 1) * P], U32, name="qc1", align_bytes=64)
-        qs1 = sb.tile([P, (PACK - 1) * P], U8, name="qs1", align_bytes=64)
-        nc.vector.quantize_mx(out=qc0[:].bitcast(FP8X4), scales=qs0[:], in_=qb0[:].rearrange("p m j -> p (m j)"))
-        nc.vector.quantize_mx(out=qc1[:].bitcast(FP8X4), scales=qs1[:], in_=qb1[:].rearrange("p r m j -> p (r m j)"))
+        for quad in range(4):
+            nc.vector.tensor_copy(
+                out=cache_plane[32 * quad : 32 * quad + 4, :].bitcast(I32), in_=scale_rows[:, quad, :]
+            )
 
         spread = {}
-        for r, width in ((0, I), (3, HALF)):
-            spread[r] = sb.tile([P, width], F32, name="spread%d" % r)
-            nc.vector.tensor_copy(out=spread[r][:], in_=factor[:, r : r + 1].to_broadcast([P, width]))
+        for r in (0, 1, 3):
+            spread[r] = sb.tile([P, HALF], F32, name="spread%d" % r)
+            nc.scalar.copy(out=spread[r][:], in_=factor[:, r : r + 1].to_broadcast([P, HALF]))
+
+        M = HALF // PACK
+        qb = [sb.tile([P, P, PACK], BF16, name="qb%d" % r, align_bytes=64) for r in range(2)]
+        qb23 = sb.tile([P, 2, P, PACK], BF16, name="qb23", align_bytes=64)
+        qb23_m = qb23[:].rearrange("p r m j -> p m r j")
+        src = [raw[c][:].rearrange("p j (m r) -> p m r j", r=PACK) for c in range(2)]
+        nc.vector.tensor_copy(out=qb[0][:, 0:M, :], in_=src[0][:, :, 0, :])
+        nc.scalar.copy(out=qb[1][:, 0:M, :], in_=src[0][:, :, 1, :])
+        nc.scalar.copy(out=qb23_m[:, 0:M], in_=src[0][:, :, 2:PACK, :])
+        for r in range(2):
+            nc.vector.tensor_copy(out=qb[r][:, M : 2 * M, :], in_=src[1][:, :, r, :])
+        nc.scalar.copy(out=qb23_m[:, M : 2 * M], in_=src[1][:, :, 2:PACK, :])
+        qc = [sb.tile([P, P], U32, name="qc%d" % r, align_bytes=64) for r in range(2)]
+        qs = [sb.tile([P, P], U8, name="qs%d" % r, align_bytes=64) for r in range(2)]
+        qc23 = sb.tile([P, 2 * P], U32, name="qc23", align_bytes=64)
+        qs23 = sb.tile([P, 2 * P], U8, name="qs23", align_bytes=64)
+        for r in range(2):
+            nc.vector.quantize_mx(out=qc[r][:].bitcast(FP8X4), scales=qs[r][:], in_=qb[r][:].rearrange("p m j -> p (m j)"))
+        f2.append(sb.tile([P, T], F32, name="qb1", align_bytes=64))
+        nc.vector.memset(f2[2][:].bitcast(I32), 0)
+        nc.vector.quantize_mx(out=qc23[:].bitcast(FP8X4), scales=qs23[:], in_=qb23[:].rearrange("p r m j -> p (r m j)"))
 
         banks = {}
         for r in range(PACK):
-            if r == 0:
-                codes, plane = qc0[:], qs0[:]
+            if r < 2:
+                codes, plane = qc[r][:], qs[r][:]
             else:
-                codes, plane = qc1[:, (r - 1) * P : r * P], qs1[:, (r - 1) * P : r * P]
-            for b in range(2):
-                banks[r, b] = psum.tile([P, BANK], F32, name="bank%d" % (2 * r + b))
+                codes, plane = qc23[:, (r - 2) * P : (r - 1) * P], qs23[:, (r - 2) * P : (r - 1) * P]
+            width = HALF if r == 0 else BANK
+            for b in range(T // width):
+                banks[r, b] = psum.tile([P, BANK], F32, name="bank%d" % ((FIRST_BANK[r] + b) % 8))
+                start = b * width
                 nc.tensor.matmul_mx(
-                    out=banks[r, b][:],
+                    out=banks[r, b][:, 0:width],
                     lhsT=codes.bitcast(FP8X4),
                     lhsT_scale=plane,
-                    rhs=keys[b][:].bitcast(FP8X4),
-                    rhs_scale=cache_plane[:, b * BANK : (b + 1) * BANK],
+                    rhs=keys[start // BANK][:, start % BANK : start % BANK + width].bitcast(FP8X4),
+                    rhs_scale=cache_plane[:, start : start + width],
                     start=True,
                     stop=True,
                 )
 
-        a = [sb.tile([P, T], F32, name="a%d" % r) for r in range(PACK)]
-        w = [sb.tile([P, I], F32, name="w%d" % r) for r in range(PACK)]
-        c1 = [sb.tile([P, T], F32, name="c1_%d" % r) for r in range(PACK)]
+        a = [sb.tile([P, T], F32, name="row%d" % r, align_bytes=64) for r in range(PACK)]
+        w = [sb.tile([P, I], F32, name="w%d" % r, align_bytes=64) for r in range(PACK)]
+        c1 = {}
         v = [sb.tile([P, J], F32, name="v%d" % r) for r in range(PACK)]
         c2 = {}
         gw = sb.tile([P, PACK, I], F32, name="gw")
 
         def leave_v(r, b):
             nc.vector.tensor_copy(out=a[r][:, b * BANK : (b + 1) * BANK], in_=banks[r, b][:])
-
-        def leave_s(r, b):
-            nc.scalar.copy(out=a[r][:, b * BANK : (b + 1) * BANK], in_=banks[r, b][:])
 
         def w_low(r):
             nc.vector.tensor_copy(w[r][:, 0:J], a[r][:].indirect(l1[:]))
@@ -137,78 +148,94 @@ def tile_attend_halfruns_one_mixed_kernel(
             nc.scalar.activation(f1[r % 2][:].indirect(l3[:]), w[r][:], COPY)
 
         def make_c1(r):
-            nc.vector.tensor_tensor(c1[r][:], a[r][:], f1[r % 2][:], ALU.subtract)
+            c1[r] = sb.tile([P, T], F32, name=("row1", "row2", "row3", "f1_0")[r], align_bytes=64)
+            if r == 0:
+                nc.vector.tensor_tensor(c1[r][:], a[r][:], f1[0][:], ALU.subtract)
+                return
+            for b in range(2):
+                cols = slice(b * BANK, (b + 1) * BANK)
+                nc.vector.tensor_tensor(c1[r][:, cols], banks[r, b][:], f1[r % 2][:, cols], ALU.subtract)
 
         def make_v(r):
             nc.vector.tensor_tensor(v[r][:], c1[r][:].indirect(l4[:]), w[r][:, 0:J], ALU.subtract)
 
         def put_v(r):
-            nc.scalar.activation(f2[r % 2][:].indirect(l2[:]), v[r][:], COPY)
+            nc.scalar.activation(f2[r % 3][:].indirect(l2[:]), v[r][:], COPY)
 
         def make_c2(r):
-            c2[r] = sb.tile([P, T], F32, name="w3" if r == 2 else "c2_%d" % r)
-            nc.vector.tensor_tensor(c2[r][:], c1[r][:], f2[r % 2][:], ALU.max)
+            c2[r] = sb.tile([P, T], F32, name=("row0", "f1_1", "w3", "row2")[r], align_bytes=64)
+            nc.vector.tensor_tensor(c2[r][:], c1[r][:], f2[r % 3][:], ALU.max)
 
-        def gw_vector(r):
-            nc.vector.tensor_tensor(gw[:, r, :], c2[r][:].indirect(l5[:]), spread[r][:], ALU.mult)
+        def gw_half_vector(r, h=0):
+            nc.vector.tensor_tensor(
+                gw[:, r, h * HALF : (h + 1) * HALF], c2[r][:].indirect(l5[:, 16 * h : 16 * (h + 1)]), spread[r][:], ALU.mult
+            )
 
-        leave_s(0, 0)
-        leave_v(0, 1)
-        w_low(0)
-        leave_s(1, 0)
+        def gw_half_scalar(r):
+            nc.scalar.activation(gw[:, r, HALF:I], c2[r][:].indirect(l5[:, 16:32]), COPY, scale=factor[:, r : r + 1])
+
+        for b in range(4):
+            copy = nc.vector.tensor_copy if b % 2 == 0 else nc.scalar.copy
+            copy(out=a[0][:, b * HALF : (b + 1) * HALF], in_=banks[0, b][:, 0:HALF])
+        nc.scalar.activation(w[0][:, 0:J], a[0][:].indirect(l1[:]), COPY)
         nc.scalar.activation(f1[0][:].indirect(l3[:, 0:16]), w[0][:, 0:J], COPY)
+        leave_v(1, 0)
         w_high(0)
         nc.scalar.activation(f1[0][:].indirect(l3[:, 16:32]), w[0][:, J:I], COPY)
         leave_v(1, 1)
+        leave_v(2, 0)
         w_low(1)
         w_high(1)
         put_w(1)
-        leave_v(2, 0)
         leave_v(2, 1)
         make_c1(0)
-        w_low(2)
+        leave_v(3, 0)
         make_v(0)
         put_v(0)
+        leave_v(3, 1)
+        w_low(2)
         w_high(2)
         put_w(2)
-        make_c1(1)
-        leave_v(3, 0)
-        make_v(1)
-        put_v(1)
-        leave_v(3, 1)
-        make_c2(0)
         w_low(3)
+        make_c1(1)
         w_high(3)
         put_w(3)
+        make_c2(0)
+        make_v(1)
+        put_v(1)
         make_c1(2)
-        make_c2(1)
-        nc.scalar.activation(gw[:, 1, :], c2[1][:].indirect(l5[:]), COPY, scale=factor[:, 1:2])
+        gw_half_vector(0, 0)
+        gw_half_vector(0, 1)
         make_v(2)
         put_v(2)
-        gw_vector(0)
         make_c1(3)
         make_v(3)
         put_v(3)
+        make_c2(1)
+        gw_half_scalar(1)
         make_c2(2)
+        gw_half_vector(1)
         nc.scalar.activation(gw[:, 2, :], c2[2][:].indirect(l5[:]), COPY, scale=factor[:, 2:3])
         make_c2(3)
-        nc.vector.tensor_tensor(gw[:, 3, 0:HALF], c2[3][:].indirect(l5[:, 0:16]), spread[3][:], ALU.mult)
-        nc.scalar.activation(gw[:, 3, HALF:I], c2[3][:].indirect(l5[:, 16:32]), COPY, scale=factor[:, 3:4])
+        gw_half_vector(3)
+        gw_half_scalar(3)
 
         gw_ir = gw[:].rearrange("p r i -> p i r")
         out_b = out.rearrange("(b p) i -> p b i", p=P)
-        gb = [sb.tile([P, HALF, PACK], BF16, name="gb%d" % h, align_bytes=64) for h in range(2)]
-        nc.vector.tensor_copy(out=gb[0][:], in_=gw_ir[:, 0:HALF, :])
-        nc.scalar.copy(out=gb[1][:], in_=gw_ir[:, HALF:I, :])
-        for h in range(2):
-            gc = sb.tile([P, HALF], U32, name="gc%d" % h, align_bytes=64)
-            gs = sb.tile([P, HALF], U8, name="gs%d" % h, align_bytes=64)
-            nc.vector.quantize_mx(out=gc[:].bitcast(FP8X4), scales=gs[:], in_=gb[h][:].rearrange("p i r -> p (i r)"))
-            res = sb.tile([P, 2, HALF], F32, name="res%d" % h)
+        gb = [sb.tile([P, P, PACK], BF16, name="gb%d" % n, align_bytes=64) for n in range(4)]
+
+        def weave(n, engine_copy):
+            engine_copy(out=gb[n][:], in_=gw_ir[:, n * P : (n + 1) * P, :])
+
+        def finish(n, last):
+            gc = sb.tile([P, P], U32, name="gc%d" % n, align_bytes=64)
+            gs = sb.tile([P, P], U8, name="gs%d" % n, align_bytes=64)
+            nc.vector.quantize_mx(out=gc[:].bitcast(FP8X4), scales=gs[:], in_=gb[n][:].rearrange("p i r -> p (i r)"))
+            res = sb.tile([P, 2, P], F32, name="res%d" % n)
             for b in range(2):
-                acc = psum.tile([P, BANK], F32, name="bank%d" % (2 * h + b))
+                acc = psum.tile([P, BANK], F32, name="bank%d" % (2 * n + b))
                 nc.tensor.matmul_mx(
-                    out=acc[:, 0:HALF],
+                    out=acc[:, 0:P],
                     lhsT=mix_codes[:, 2 * P * b : 2 * P * (b + 1)].bitcast(FP4X4),
                     lhsT_scale=mix_plane[:, P * b : P * (b + 1)],
                     rhs=gc[:].bitcast(FP8X4),
@@ -216,8 +243,17 @@ def tile_attend_halfruns_one_mixed_kernel(
                     start=True,
                     stop=True,
                 )
-                if b == 0:
-                    nc.vector.tensor_copy(out=res[:, b, :], in_=acc[:, 0:HALF])
+                if last and b == 0:
+                    nc.vector.tensor_copy(out=res[:, b, :], in_=acc[:, 0:P])
                 else:
-                    nc.scalar.copy(out=res[:, b, :], in_=acc[:, 0:HALF])
-            nc.sync.dma_start(out=out_b[:, :, h * HALF : (h + 1) * HALF], in_=res[:])
+                    nc.scalar.copy(out=res[:, b, :], in_=acc[:, 0:P])
+            nc.sync.dma_start(out=out_b[:, :, n * P : (n + 1) * P], in_=res[:])
+
+        weave(0, nc.vector.tensor_copy)
+        weave(1, nc.vector.tensor_copy)
+        weave(2, nc.scalar.copy)
+        finish(0, False)
+        finish(2, False)
+        weave(3, nc.vector.tensor_copy)
+        finish(1, True)
+        finish(3, True)

@@ -20,12 +20,17 @@ P = 128
 PACK = 4
 BANK = 512
 HALF = 256
-FIRST_BANK = (0, 4, 6, 0)
+LIST_HALF = HALF // 16
+
+FIRST_BANK = (0, 0, 2, 4)
+
+C1_BUFFER = ("row1", "row2", "row3", "f1_0")
+C2_BUFFER = ("row0", "f1_1", "w3", "row2")
 
 
-def load_scale_rows(queue, plane, rows):
+def load_scale_rows(nc, plane, rows):
     for quad in range(4):
-        queue.dma_start(
+        nc.sync.dma_start(
             out=plane[32 * quad : 32 * quad + 4, :].bitcast(I32),
             in_=rows[4 * quad : 4 * quad + 4, :].bitcast(I32),
         )
@@ -47,40 +52,32 @@ def tile_attend_halfruns_one_mixed_kernel(
 
         factor = sb.tile([P, PACK], F32, name="factor")
         nc.sync.dma_start(out=factor[:], in_=rowf.rearrange("(p r) o -> p (r o)", r=PACK))
-        scale_rows = sb.tile([4, 4, T // 4], I32, name="scale_rows")
-        nc.sync.dma_start(out=scale_rows[:], in_=cache_scales[0].bitcast(I32).rearrange("(quad f) c -> f quad c", f=4))
-        query_pj = query.rearrange("(p j) q -> p j q", j=PACK)
+        query_by_place = query.rearrange("(p j) q -> p j q", j=PACK)
         raw = [sb.tile([P, PACK, HALF], F32, name="raw%d" % c) for c in range(2)]
         for c in range(2):
-            nc.sync.dma_start(out=raw[c][:], in_=query_pj[:, :, c * HALF : (c + 1) * HALF])
-        words_flat = cache_words[0].rearrange("p n t -> p (n t)")
-        keys = [sb.tile([P, BANK], I32, name="keys%d" % b, align_bytes=64) for b in range(2)]
-        for b in range(2):
-            nc.sync.dma_start(out=keys[b][:], in_=words_flat[:, b * BANK * PACK : (b + 1) * BANK * PACK].bitcast(I32))
+            nc.sync.dma_start(out=raw[c][:], in_=query_by_place[:, :, c * HALF : (c + 1) * HALF])
+        load_scale_rows(nc, cache_plane, cache_scales[0])
+        keys = sb.tile([P, T], I32, name="keys", align_bytes=64)
+        nc.sync.dma_start(out=keys[:], in_=cache_words[0].rearrange("p n t -> p (n t)").bitcast(I32))
 
-        l1 = lists.tile([P, J // 16], U16, name="l1")
-        l2 = lists.tile([P, J // 16], U16, name="l2")
-        l3 = lists.tile([P, I // 16], U16, name="l3")
-        l4 = lists.tile([P, J // 16], U16, name="l4")
-        l5 = lists.tile([P, I // 16], U16, name="l5")
-        nc.sync.dma_start(l1[:], offs)
-        nc.sync.dma_start(l3[:], offs3)
-        nc.sync.dma_start(l2[:], offs2)
-        nc.sync.dma_start(l4[:], offs4)
-        nc.sync.dma_start(l5[:], offs5)
+        idx = lists.tile([P, J // 16], U16, name="idx")
+        idx2 = lists.tile([P, J // 16], U16, name="idx2")
+        idx3 = lists.tile([P, I // 16], U16, name="idx3")
+        idx4 = lists.tile([P, J // 16], U16, name="idx4")
+        idx5 = lists.tile([P, I // 16], U16, name="idx5")
+        nc.sync.dma_start(idx[:], offs)
+        nc.sync.dma_start(idx3[:], offs3)
+        nc.sync.dma_start(idx2[:], offs2)
+        nc.sync.dma_start(idx4[:], offs4)
+        nc.sync.dma_start(idx5[:], offs5)
         mix_codes = sb.tile([P, 2 * E], U8, name="mix_codes", align_bytes=64)
         nc.sync.dma_start(out=mix_codes[:].bitcast(I32), in_=mix_words[0].bitcast(I32))
-        load_scale_rows(nc.sync, mix_plane, mix_scales[0])
+        load_scale_rows(nc, mix_plane, mix_scales[0])
 
         f1 = [sb.tile([P, T], F32, name="f1_%d" % s, align_bytes=64) for s in range(2)]
         f2 = [sb.tile([P, T], F32, name="f2_%d" % s) for s in range(2)]
         for window in f1 + f2:
             nc.vector.memset(window[:].bitcast(I32), 0)
-
-        for quad in range(4):
-            nc.vector.tensor_copy(
-                out=cache_plane[32 * quad : 32 * quad + 4, :].bitcast(I32), in_=scale_rows[:, quad, :]
-            )
 
         spread = {}
         for r in (0, 1, 3):
@@ -88,42 +85,47 @@ def tile_attend_halfruns_one_mixed_kernel(
             nc.scalar.copy(out=spread[r][:], in_=factor[:, r : r + 1].to_broadcast([P, HALF]))
 
         M = HALF // PACK
-        qb = [sb.tile([P, P, PACK], BF16, name="qb%d" % r, align_bytes=64) for r in range(2)]
-        qb23 = sb.tile([P, 2, P, PACK], BF16, name="qb23", align_bytes=64)
-        qb23_m = qb23[:].rearrange("p r m j -> p m r j")
-        src = [raw[c][:].rearrange("p j (m r) -> p m r j", r=PACK) for c in range(2)]
-        nc.vector.tensor_copy(out=qb[0][:, 0:M, :], in_=src[0][:, :, 0, :])
-        nc.scalar.copy(out=qb[1][:, 0:M, :], in_=src[0][:, :, 1, :])
-        nc.scalar.copy(out=qb23_m[:, 0:M], in_=src[0][:, :, 2:PACK, :])
+        cast = [sb.tile([P, P, PACK], BF16, name="cast%d" % r, align_bytes=64) for r in range(2)]
+        cast23 = sb.tile([P, 2, P, PACK], BF16, name="cast23", align_bytes=64)
+        cast23_by_column = cast23[:].rearrange("p r m j -> p m r j")
+        dealt = [raw[c][:].rearrange("p j (m r) -> p m r j", r=PACK) for c in range(2)]
+        nc.vector.tensor_copy(out=cast[0][:, 0:M, :], in_=dealt[0][:, :, 0, :])
+        nc.scalar.copy(out=cast[1][:, 0:M, :], in_=dealt[0][:, :, 1, :])
+        nc.scalar.copy(out=cast23_by_column[:, 0:M], in_=dealt[0][:, :, 2:PACK, :])
         for r in range(2):
-            nc.vector.tensor_copy(out=qb[r][:, M : 2 * M, :], in_=src[1][:, :, r, :])
-        nc.scalar.copy(out=qb23_m[:, M : 2 * M], in_=src[1][:, :, 2:PACK, :])
-        qc = [sb.tile([P, P], U32, name="qc%d" % r, align_bytes=64) for r in range(2)]
-        qs = [sb.tile([P, P], U8, name="qs%d" % r, align_bytes=64) for r in range(2)]
-        qc23 = sb.tile([P, 2 * P], U32, name="qc23", align_bytes=64)
-        qs23 = sb.tile([P, 2 * P], U8, name="qs23", align_bytes=64)
+            nc.vector.tensor_copy(out=cast[r][:, M : 2 * M, :], in_=dealt[1][:, :, r, :])
+        nc.scalar.copy(out=cast23_by_column[:, M : 2 * M], in_=dealt[1][:, :, 2:PACK, :])
+        q_codes = [sb.tile([P, P], U32, name="q_codes%d" % r, align_bytes=64) for r in range(2)]
+        q_plane = [sb.tile([P, P], U8, name="q_plane%d" % r, align_bytes=64) for r in range(2)]
+        q_codes23 = sb.tile([P, 2 * P], U32, name="q_codes23", align_bytes=64)
+        q_plane23 = sb.tile([P, 2 * P], U8, name="q_plane23", align_bytes=64)
         for r in range(2):
-            nc.vector.quantize_mx(out=qc[r][:].bitcast(FP8X4), scales=qs[r][:], in_=qb[r][:].rearrange("p m j -> p (m j)"))
-        f2.append(sb.tile([P, T], F32, name="qb1", align_bytes=64))
+            nc.vector.quantize_mx(
+                out=q_codes[r][:].bitcast(FP8X4), scales=q_plane[r][:], in_=cast[r][:].rearrange("p m j -> p (m j)")
+            )
+        f2.append(sb.tile([P, T], F32, name="cast1", align_bytes=64))
         nc.vector.memset(f2[2][:].bitcast(I32), 0)
-        nc.vector.quantize_mx(out=qc23[:].bitcast(FP8X4), scales=qs23[:], in_=qb23[:].rearrange("p r m j -> p (r m j)"))
+        nc.vector.quantize_mx(
+            out=q_codes23[:].bitcast(FP8X4), scales=q_plane23[:], in_=cast23[:].rearrange("p r m j -> p (r m j)")
+        )
 
         banks = {}
-        for r in range(PACK):
+
+        def score(r):
             if r < 2:
-                codes, plane = qc[r][:], qs[r][:]
+                codes, plane = q_codes[r][:], q_plane[r][:]
             else:
-                codes, plane = qc23[:, (r - 2) * P : (r - 1) * P], qs23[:, (r - 2) * P : (r - 1) * P]
+                codes, plane = q_codes23[:, (r - 2) * P : (r - 1) * P], q_plane23[:, (r - 2) * P : (r - 1) * P]
             width = HALF if r == 0 else BANK
             for b in range(T // width):
-                banks[r, b] = psum.tile([P, BANK], F32, name="bank%d" % ((FIRST_BANK[r] + b) % 8))
-                start = b * width
+                banks[r, b] = psum.tile([P, BANK], F32, name="bank%d" % (FIRST_BANK[r] + b))
+                first_token = b * width
                 nc.tensor.matmul_mx(
                     out=banks[r, b][:, 0:width],
                     lhsT=codes.bitcast(FP8X4),
                     lhsT_scale=plane,
-                    rhs=keys[start // BANK][:, start % BANK : start % BANK + width].bitcast(FP8X4),
-                    rhs_scale=cache_plane[:, start : start + width],
+                    rhs=keys[:, first_token : first_token + width].bitcast(FP8X4),
+                    rhs_scale=cache_plane[:, first_token : first_token + width],
                     start=True,
                     stop=True,
                 )
@@ -135,20 +137,20 @@ def tile_attend_halfruns_one_mixed_kernel(
         c2 = {}
         gw = sb.tile([P, PACK, I], F32, name="gw")
 
-        def leave_v(r, b):
+        def leave_bank(r, b):
             nc.vector.tensor_copy(out=a[r][:, b * BANK : (b + 1) * BANK], in_=banks[r, b][:])
 
         def w_low(r):
-            nc.vector.tensor_copy(w[r][:, 0:J], a[r][:].indirect(l1[:]))
+            nc.vector.tensor_copy(w[r][:, 0:J], a[r][:].indirect(idx[:]))
 
         def w_high(r):
-            nc.vector.tensor_copy(w[r][:, J:I], a[r][:].indirect(l2[:]))
+            nc.vector.tensor_copy(w[r][:, J:I], a[r][:].indirect(idx2[:]))
 
-        def put_w(r):
-            nc.scalar.activation(f1[r % 2][:].indirect(l3[:]), w[r][:], COPY)
+        def scatter_w(r):
+            nc.scalar.activation(f1[r % 2][:].indirect(idx3[:]), w[r][:], COPY)
 
         def make_c1(r):
-            c1[r] = sb.tile([P, T], F32, name=("row1", "row2", "row3", "f1_0")[r], align_bytes=64)
+            c1[r] = sb.tile([P, T], F32, name=C1_BUFFER[r], align_bytes=64)
             if r == 0:
                 nc.vector.tensor_tensor(c1[r][:], a[r][:], f1[0][:], ALU.subtract)
                 return
@@ -157,97 +159,107 @@ def tile_attend_halfruns_one_mixed_kernel(
                 nc.vector.tensor_tensor(c1[r][:, cols], banks[r, b][:], f1[r % 2][:, cols], ALU.subtract)
 
         def make_v(r):
-            nc.vector.tensor_tensor(v[r][:], c1[r][:].indirect(l4[:]), w[r][:, 0:J], ALU.subtract)
+            nc.vector.tensor_tensor(v[r][:], c1[r][:].indirect(idx4[:]), w[r][:, 0:J], ALU.subtract)
 
-        def put_v(r):
-            nc.scalar.activation(f2[r % 3][:].indirect(l2[:]), v[r][:], COPY)
+        def scatter_v(r):
+            nc.scalar.activation(f2[r % 3][:].indirect(idx2[:]), v[r][:], COPY)
 
         def make_c2(r):
-            c2[r] = sb.tile([P, T], F32, name=("row0", "f1_1", "w3", "row2")[r], align_bytes=64)
+            c2[r] = sb.tile([P, T], F32, name=C2_BUFFER[r], align_bytes=64)
             nc.vector.tensor_tensor(c2[r][:], c1[r][:], f2[r % 3][:], ALU.max)
 
-        def gw_half_vector(r, h=0):
+        def gw_vector(r, half):
+            entries = idx5[:, half * LIST_HALF : (half + 1) * LIST_HALF]
             nc.vector.tensor_tensor(
-                gw[:, r, h * HALF : (h + 1) * HALF], c2[r][:].indirect(l5[:, 16 * h : 16 * (h + 1)]), spread[r][:], ALU.mult
+                gw[:, r, half * HALF : (half + 1) * HALF], c2[r][:].indirect(entries), spread[r][:], ALU.mult
             )
 
-        def gw_half_scalar(r):
-            nc.scalar.activation(gw[:, r, HALF:I], c2[r][:].indirect(l5[:, 16:32]), COPY, scale=factor[:, r : r + 1])
+        def gw_scalar(r, first_half):
+            entries = idx5[:, first_half * LIST_HALF : 2 * LIST_HALF]
+            nc.scalar.activation(
+                gw[:, r, first_half * HALF : I], c2[r][:].indirect(entries), COPY, scale=factor[:, r : r + 1]
+            )
 
-        for b in range(4):
+        score(0)
+        for b in range(T // HALF):
             copy = nc.vector.tensor_copy if b % 2 == 0 else nc.scalar.copy
             copy(out=a[0][:, b * HALF : (b + 1) * HALF], in_=banks[0, b][:, 0:HALF])
-        nc.scalar.activation(w[0][:, 0:J], a[0][:].indirect(l1[:]), COPY)
-        nc.scalar.activation(f1[0][:].indirect(l3[:, 0:16]), w[0][:, 0:J], COPY)
-        leave_v(1, 0)
+        for r in range(1, PACK):
+            score(r)
+        nc.scalar.activation(w[0][:, 0:J], a[0][:].indirect(idx[:]), COPY)
+        nc.scalar.activation(f1[0][:].indirect(idx3[:, 0:LIST_HALF]), w[0][:, 0:J], COPY)
+        leave_bank(1, 0)
         w_high(0)
-        nc.scalar.activation(f1[0][:].indirect(l3[:, 16:32]), w[0][:, J:I], COPY)
-        leave_v(1, 1)
-        leave_v(2, 0)
+        nc.scalar.activation(f1[0][:].indirect(idx3[:, LIST_HALF : 2 * LIST_HALF]), w[0][:, J:I], COPY)
+
+        leave_bank(1, 1)
+        leave_bank(2, 0)
         w_low(1)
         w_high(1)
-        put_w(1)
-        leave_v(2, 1)
+        scatter_w(1)
+        leave_bank(2, 1)
         make_c1(0)
-        leave_v(3, 0)
+        leave_bank(3, 0)
         make_v(0)
-        put_v(0)
-        leave_v(3, 1)
+        scatter_v(0)
+        leave_bank(3, 1)
         w_low(2)
         w_high(2)
-        put_w(2)
+        scatter_w(2)
         w_low(3)
         make_c1(1)
         w_high(3)
-        put_w(3)
+        scatter_w(3)
         make_c2(0)
         make_v(1)
-        put_v(1)
+        scatter_v(1)
         make_c1(2)
-        gw_half_vector(0, 0)
-        gw_half_vector(0, 1)
+        gw_vector(0, 0)
+        gw_vector(0, 1)
         make_v(2)
-        put_v(2)
+        scatter_v(2)
         make_c1(3)
         make_v(3)
-        put_v(3)
+        scatter_v(3)
         make_c2(1)
-        gw_half_scalar(1)
+        gw_scalar(1, 1)
         make_c2(2)
-        gw_half_vector(1)
-        nc.scalar.activation(gw[:, 2, :], c2[2][:].indirect(l5[:]), COPY, scale=factor[:, 2:3])
+        gw_vector(1, 0)
+        gw_scalar(2, 0)
         make_c2(3)
-        gw_half_vector(3)
-        gw_half_scalar(3)
+        gw_vector(3, 0)
+        gw_scalar(3, 1)
 
-        gw_ir = gw[:].rearrange("p r i -> p i r")
-        out_b = out.rearrange("(b p) i -> p b i", p=P)
-        gb = [sb.tile([P, P, PACK], BF16, name="gb%d" % n, align_bytes=64) for n in range(4)]
+        gw_by_slot = gw[:].rearrange("p r i -> p i r")
+        out_by_block = out.rearrange("(b p) i -> p b i", p=P)
+        woven = [sb.tile([P, P, PACK], BF16, name="woven%d" % n, align_bytes=64) for n in range(I // P)]
 
         def weave(n, engine_copy):
-            engine_copy(out=gb[n][:], in_=gw_ir[:, n * P : (n + 1) * P, :])
+            engine_copy(out=woven[n][:], in_=gw_by_slot[:, n * P : (n + 1) * P, :])
 
-        def finish(n, last):
-            gc = sb.tile([P, P], U32, name="gc%d" % n, align_bytes=64)
-            gs = sb.tile([P, P], U8, name="gs%d" % n, align_bytes=64)
-            nc.vector.quantize_mx(out=gc[:].bitcast(FP8X4), scales=gs[:], in_=gb[n][:].rearrange("p i r -> p (i r)"))
-            res = sb.tile([P, 2, P], F32, name="res%d" % n)
-            for b in range(2):
+        def finish(n, shared):
+            g_codes = sb.tile([P, P], U32, name="g_codes%d" % n, align_bytes=64)
+            g_plane = sb.tile([P, P], U8, name="g_plane%d" % n, align_bytes=64)
+            nc.vector.quantize_mx(
+                out=g_codes[:].bitcast(FP8X4), scales=g_plane[:], in_=woven[n][:].rearrange("p i r -> p (i r)")
+            )
+            result = sb.tile([P, E // P, P], F32, name="result%d" % n)
+            for b in range(E // P):
                 acc = psum.tile([P, BANK], F32, name="bank%d" % (2 * n + b))
                 nc.tensor.matmul_mx(
                     out=acc[:, 0:P],
                     lhsT=mix_codes[:, 2 * P * b : 2 * P * (b + 1)].bitcast(FP4X4),
                     lhsT_scale=mix_plane[:, P * b : P * (b + 1)],
-                    rhs=gc[:].bitcast(FP8X4),
-                    rhs_scale=gs[:],
+                    rhs=g_codes[:].bitcast(FP8X4),
+                    rhs_scale=g_plane[:],
                     start=True,
                     stop=True,
                 )
-                if last and b == 0:
-                    nc.vector.tensor_copy(out=res[:, b, :], in_=acc[:, 0:P])
+                if shared and b == 0:
+                    nc.vector.tensor_copy(out=result[:, b, :], in_=acc[:, 0:P])
                 else:
-                    nc.scalar.copy(out=res[:, b, :], in_=acc[:, 0:P])
-            nc.sync.dma_start(out=out_b[:, :, n * P : (n + 1) * P], in_=res[:])
+                    nc.scalar.copy(out=result[:, b, :], in_=acc[:, 0:P])
+            nc.sync.dma_start(out=out_by_block[:, :, n * P : (n + 1) * P], in_=result[:])
 
         weave(0, nc.vector.tensor_copy)
         weave(1, nc.vector.tensor_copy)

from contextlib import ExitStack

import concourse.mybir as mybir

D, T, I, J, Q, E = 512, 1024, 512, 256, 512, 256
FLOPS = 2 * D * Q * T + 2 * Q * E * I

F32 = mybir.dt.float32
BF16 = mybir.dt.bfloat16
I32 = mybir.dt.int32
U32 = mybir.dt.uint32
U16 = mybir.dt.uint16
U8 = mybir.dt.uint8
FP8X4 = mybir.dt.float8_e4m3fn_x4
FP4X4 = mybir.dt.float4_e2m1fn_x4
ALU = mybir.AluOpType
COPY = mybir.ActivationFunctionType.Copy

P = 128
PACK = 4
BANK = 512
HALF = 256
LIST_HALF = HALF // 16

FIRST_BANK = (0, 0, 2, 4)

C1_BUFFER = ("row1", "row2", "row3", "f1_0")
C2_BUFFER = ("row0", "f1_1", "w3", "row2")


def load_scale_rows(nc, plane, rows):
    for quad in range(4):
        nc.sync.dma_start(
            out=plane[32 * quad : 32 * quad + 4, :].bitcast(I32),
            in_=rows[4 * quad : 4 * quad + 4, :].bitcast(I32),
        )


def tile_attend_halfruns_one_mixed_kernel(
    tc, query, cache_words, cache_scales, rowf, mix_words, mix_scales, offs, offs2, offs3, offs4, offs5, out
):
    nc = tc.nc
    with ExitStack() as ctx:
        lists = ctx.enter_context(tc.tile_pool(name="lists", bufs=1))
        sb = ctx.enter_context(tc.tile_pool(name="sb", bufs=1))
        psum = ctx.enter_context(tc.psum_pool(name="psum", bufs=1))

        cache_plane = sb.tile([P, T], U8, name="cache_plane", align_bytes=64)
        mix_plane = sb.tile([P, E], U8, name="mix_plane", align_bytes=64)
        nc.vector.memset(cache_plane[:].bitcast(I32), 0)
        nc.vector.memset(mix_plane[:].bitcast(I32), 0)

        factor = sb.tile([P, PACK], F32, name="factor")
        nc.sync.dma_start(out=factor[:], in_=rowf.rearrange("(p r) o -> p (r o)", r=PACK))
        query_by_place = query.rearrange("(p j) q -> p j q", j=PACK)
        raw = [sb.tile([P, PACK, HALF], F32, name="raw%d" % c) for c in range(2)]
        for c in range(2):
            nc.sync.dma_start(out=raw[c][:], in_=query_by_place[:, :, c * HALF : (c + 1) * HALF])
        load_scale_rows(nc, cache_plane, cache_scales[0])
        keys = sb.tile([P, T], I32, name="keys", align_bytes=64)
        nc.sync.dma_start(out=keys[:], in_=cache_words[0].rearrange("p n t -> p (n t)").bitcast(I32))

        idx = lists.tile([P, J // 16], U16, name="idx")
        idx2 = lists.tile([P, J // 16], U16, name="idx2")
        idx3 = lists.tile([P, I // 16], U16, name="idx3")
        idx4 = lists.tile([P, J // 16], U16, name="idx4")
        idx5 = lists.tile([P, I // 16], U16, name="idx5")
        nc.sync.dma_start(idx[:], offs)
        nc.sync.dma_start(idx3[:], offs3)
        nc.sync.dma_start(idx2[:], offs2)
        nc.sync.dma_start(idx4[:], offs4)
        nc.sync.dma_start(idx5[:], offs5)
        mix_codes = sb.tile([P, 2 * E], U8, name="mix_codes", align_bytes=64)
        nc.sync.dma_start(out=mix_codes[:].bitcast(I32), in_=mix_words[0].bitcast(I32))
        load_scale_rows(nc, mix_plane, mix_scales[0])

        f1 = [sb.tile([P, T], F32, name="f1_%d" % s, align_bytes=64) for s in range(2)]
        f2 = [sb.tile([P, T], F32, name="f2_%d" % s) for s in range(2)]
        for window in f1 + f2:
            nc.vector.memset(window[:].bitcast(I32), 0)

        spread = {}
        for r in (0, 1, 3):
            spread[r] = sb.tile([P, HALF], F32, name="spread%d" % r)
            nc.scalar.copy(out=spread[r][:], in_=factor[:, r : r + 1].to_broadcast([P, HALF]))

        M = HALF // PACK
        cast = [sb.tile([P, P, PACK], BF16, name="cast%d" % r, align_bytes=64) for r in range(2)]
        cast23 = sb.tile([P, 2, P, PACK], BF16, name="cast23", align_bytes=64)
        cast23_by_column = cast23[:].rearrange("p r m j -> p m r j")
        dealt = [raw[c][:].rearrange("p j (m r) -> p m r j", r=PACK) for c in range(2)]
        nc.vector.tensor_copy(out=cast[0][:, 0:M, :], in_=dealt[0][:, :, 0, :])
        nc.scalar.copy(out=cast[1][:, 0:M, :], in_=dealt[0][:, :, 1, :])
        nc.scalar.copy(out=cast23_by_column[:, 0:M], in_=dealt[0][:, :, 2:PACK, :])
        for r in range(2):
            nc.vector.tensor_copy(out=cast[r][:, M : 2 * M, :], in_=dealt[1][:, :, r, :])
        nc.scalar.copy(out=cast23_by_column[:, M : 2 * M], in_=dealt[1][:, :, 2:PACK, :])
        q_codes = [sb.tile([P, P], U32, name="q_codes%d" % r, align_bytes=64) for r in range(2)]
        q_plane = [sb.tile([P, P], U8, name="q_plane%d" % r, align_bytes=64) for r in range(2)]
        q_codes23 = sb.tile([P, 2 * P], U32, name="q_codes23", align_bytes=64)
        q_plane23 = sb.tile([P, 2 * P], U8, name="q_plane23", align_bytes=64)
        for r in range(2):
            nc.vector.quantize_mx(
                out=q_codes[r][:].bitcast(FP8X4), scales=q_plane[r][:], in_=cast[r][:].rearrange("p m j -> p (m j)")
            )
        f2.append(sb.tile([P, T], F32, name="cast1", align_bytes=64))
        nc.vector.memset(f2[2][:].bitcast(I32), 0)
        nc.vector.quantize_mx(
            out=q_codes23[:].bitcast(FP8X4), scales=q_plane23[:], in_=cast23[:].rearrange("p r m j -> p (r m j)")
        )

        banks = {}

        def score(r):
            if r < 2:
                codes, plane = q_codes[r][:], q_plane[r][:]
            else:
                codes, plane = q_codes23[:, (r - 2) * P : (r - 1) * P], q_plane23[:, (r - 2) * P : (r - 1) * P]
            width = HALF if r == 0 else BANK
            for b in range(T // width):
                banks[r, b] = psum.tile([P, BANK], F32, name="bank%d" % (FIRST_BANK[r] + b))
                first_token = b * width
                nc.tensor.matmul_mx(
                    out=banks[r, b][:, 0:width],
                    lhsT=codes.bitcast(FP8X4),
                    lhsT_scale=plane,
                    rhs=keys[:, first_token : first_token + width].bitcast(FP8X4),
                    rhs_scale=cache_plane[:, first_token : first_token + width],
                    start=True,
                    stop=True,
                )

        a = [sb.tile([P, T], F32, name="row%d" % r, align_bytes=64) for r in range(PACK)]
        w = [sb.tile([P, I], F32, name="w%d" % r, align_bytes=64) for r in range(PACK)]
        c1 = {}
        v = [sb.tile([P, J], F32, name="v%d" % r) for r in range(PACK)]
        c2 = {}
        gw = sb.tile([P, PACK, I], F32, name="gw")

        def leave_bank(r, b):
            nc.vector.tensor_copy(out=a[r][:, b * BANK : (b + 1) * BANK], in_=banks[r, b][:])

        def w_low(r):
            nc.vector.tensor_copy(w[r][:, 0:J], a[r][:].indirect(idx[:]))

        def w_high(r):
            nc.vector.tensor_copy(w[r][:, J:I], a[r][:].indirect(idx2[:]))

        def scatter_w(r):
            nc.scalar.activation(f1[r % 2][:].indirect(idx3[:]), w[r][:], COPY)

        def make_c1(r):
            c1[r] = sb.tile([P, T], F32, name=C1_BUFFER[r], align_bytes=64)
            if r == 0:
                nc.vector.tensor_tensor(c1[r][:], a[r][:], f1[0][:], ALU.subtract)
                return
            for b in range(2):
                cols = slice(b * BANK, (b + 1) * BANK)
                nc.vector.tensor_tensor(c1[r][:, cols], banks[r, b][:], f1[r % 2][:, cols], ALU.subtract)

        def make_v(r):
            nc.vector.tensor_tensor(v[r][:], c1[r][:].indirect(idx4[:]), w[r][:, 0:J], ALU.subtract)

        def scatter_v(r):
            nc.scalar.activation(f2[r % 3][:].indirect(idx2[:]), v[r][:], COPY)

        def make_c2(r):
            c2[r] = sb.tile([P, T], F32, name=C2_BUFFER[r], align_bytes=64)
            nc.vector.tensor_tensor(c2[r][:], c1[r][:], f2[r % 3][:], ALU.max)

        def gw_vector(r, half):
            entries = idx5[:, half * LIST_HALF : (half + 1) * LIST_HALF]
            nc.vector.tensor_tensor(
                gw[:, r, half * HALF : (half + 1) * HALF], c2[r][:].indirect(entries), spread[r][:], ALU.mult
            )

        def gw_scalar(r, first_half):
            entries = idx5[:, first_half * LIST_HALF : 2 * LIST_HALF]
            nc.scalar.activation(
                gw[:, r, first_half * HALF : I], c2[r][:].indirect(entries), COPY, scale=factor[:, r : r + 1]
            )

        score(0)
        for b in range(T // HALF):
            copy = nc.vector.tensor_copy if b % 2 == 0 else nc.scalar.copy
            copy(out=a[0][:, b * HALF : (b + 1) * HALF], in_=banks[0, b][:, 0:HALF])
        for r in range(1, PACK):
            score(r)
        nc.scalar.activation(w[0][:, 0:J], a[0][:].indirect(idx[:]), COPY)
        nc.scalar.activation(f1[0][:].indirect(idx3[:, 0:LIST_HALF]), w[0][:, 0:J], COPY)
        leave_bank(1, 0)
        w_high(0)
        nc.scalar.activation(f1[0][:].indirect(idx3[:, LIST_HALF : 2 * LIST_HALF]), w[0][:, J:I], COPY)

        leave_bank(1, 1)
        leave_bank(2, 0)
        w_low(1)
        w_high(1)
        scatter_w(1)
        leave_bank(2, 1)
        make_c1(0)
        leave_bank(3, 0)
        make_v(0)
        scatter_v(0)
        leave_bank(3, 1)
        w_low(2)
        w_high(2)
        scatter_w(2)
        w_low(3)
        make_c1(1)
        w_high(3)
        scatter_w(3)
        make_c2(0)
        make_v(1)
        scatter_v(1)
        make_c1(2)
        gw_vector(0, 0)
        gw_vector(0, 1)
        make_v(2)
        scatter_v(2)
        make_c1(3)
        make_v(3)
        scatter_v(3)
        make_c2(1)
        gw_scalar(1, 1)
        make_c2(2)
        gw_vector(1, 0)
        gw_scalar(2, 0)
        make_c2(3)
        gw_vector(3, 0)
        gw_scalar(3, 1)

        gw_by_slot = gw[:].rearrange("p r i -> p i r")
        out_by_block = out.rearrange("(b p) i -> p b i", p=P)
        woven = [sb.tile([P, P, PACK], BF16, name="woven%d" % n, align_bytes=64) for n in range(I // P)]

        def weave(n, engine_copy):
            engine_copy(out=woven[n][:], in_=gw_by_slot[:, n * P : (n + 1) * P, :])

        def finish(n, shared):
            g_codes = sb.tile([P, P], U32, name="g_codes%d" % n, align_bytes=64)
            g_plane = sb.tile([P, P], U8, name="g_plane%d" % n, align_bytes=64)
            nc.vector.quantize_mx(
                out=g_codes[:].bitcast(FP8X4), scales=g_plane[:], in_=woven[n][:].rearrange("p i r -> p (i r)")
            )
            result = sb.tile([P, E // P, P], F32, name="result%d" % n)
            for b in range(E // P):
                acc = psum.tile([P, BANK], F32, name="bank%d" % (2 * n + b))
                nc.tensor.matmul_mx(
                    out=acc[:, 0:P],
                    lhsT=mix_codes[:, 2 * P * b : 2 * P * (b + 1)].bitcast(FP4X4),
                    lhsT_scale=mix_plane[:, P * b : P * (b + 1)],
                    rhs=g_codes[:].bitcast(FP8X4),
                    rhs_scale=g_plane[:],
                    start=True,
                    stop=True,
                )
                if shared and b == 0:
                    nc.vector.tensor_copy(out=result[:, b, :], in_=acc[:, 0:P])
                else:
                    nc.scalar.copy(out=result[:, b, :], in_=acc[:, 0:P])
            nc.sync.dma_start(out=out_by_block[:, :, n * P : (n + 1) * P], in_=result[:])

        weave(0, nc.vector.tensor_copy)
        weave(1, nc.vector.tensor_copy)
        weave(2, nc.scalar.copy)
        finish(0, False)
        finish(2, False)
        weave(3, nc.vector.tensor_copy)
        finish(1, True)
        finish(3, True)
